import numpy as np
import ml_dtypes


def mxq(x, axis, fmt="e4m3"):
    dtype, down = {"e4m3": (ml_dtypes.float8_e4m3fn, 7), "e5m2": (ml_dtypes.float8_e5m2, 14)}[fmt]
    v = np.moveaxis(np.asarray(x, np.float32).astype(ml_dtypes.bfloat16).astype(np.float64), axis, -1)
    blocks = v.reshape(v.shape[:-1] + (-1, 32))
    amax = np.abs(blocks).max(-1, keepdims=True)
    byte = np.maximum(np.where(amax > 0, np.frexp(amax)[1] - 1 + 127, 0) - down, 1)
    scale = np.exp2(byte - 127.0)
    codes = (blocks / scale).astype(np.float32).astype(dtype).astype(np.float64)
    return np.moveaxis((codes * scale).reshape(v.shape), -1, axis)


WIDE = False


def mx_kscale(k):
    if not WIDE:
        return np.ones(k)
    levels = np.array([24, -24, 12, -12, 0])
    if k % 512:
        return np.exp2(np.random.permutation(np.resize(levels, k // 32))).repeat(32)
    a = np.empty((k // 512, 16))
    for p in range(k // 512):
        a[p, :8] = np.random.permutation(np.resize(levels, 8))
        for g in range(8):
            far = levels[np.abs(levels - a[p, g]) >= 10]
            a[p, g + 8] = far[np.random.randint(len(far))]
    return np.exp2(a.ravel()).repeat(32)


def f64(x):
    return np.asarray(x).astype(np.float64)


E2M1 = np.array([0.0, 0.5, 1.0, 1.5, 2.0, 3.0, 4.0, 6.0, -0.0, -0.5, -1.0, -1.5, -2.0, -3.0, -4.0, -6.0])


def pack_weight(w, fmt):
    k, n = w.shape
    w = f64(np.asarray(w, np.float32).astype(ml_dtypes.bfloat16)).reshape(k // 32, 32, n)
    amax = np.abs(w).max(1)
    if fmt == "e4m3":
        byte = np.frexp(amax)[1] - 1 + 127 - 7
    else:
        mant, ex = np.frexp(amax / 6.0)
        byte = np.where(mant > 0.5, ex, ex - 1) + 127
    byte = np.clip(np.where(amax > 0, byte, 1), 1, 254)
    scaled = (w * np.exp2(127.0 - byte)[:, None, :]).reshape(k, n).astype(np.float32)
    by_word = np.ascontiguousarray(scaled.reshape(k // 512, 128, 4, n).transpose(0, 1, 3, 2))
    if fmt == "e4m3":
        words = by_word.astype(ml_dtypes.float8_e4m3fn).view(np.uint8)
    else:
        c = by_word.astype(ml_dtypes.float4_e2m1fn).view(np.uint8) & 0xF
        words = (c[..., 0::2] | (c[..., 1::2] << 4)).reshape(k // 512, 128, 2 * n)
    return np.ascontiguousarray(words), np.ascontiguousarray(byte.astype(np.uint8).reshape(k // 512, 16, n))


def unpack_weight(words, scales, fmt):
    g, _, n = scales.shape
    words = np.ascontiguousarray(words).reshape(g, 128, n, -1)
    if fmt == "e4m3":
        vals = words.view(ml_dtypes.float8_e4m3fn).astype(np.float64)
    else:
        nib = np.empty((g, 128, n, 4), np.uint8)
        nib[..., 0::2] = words & 0xF
        nib[..., 1::2] = words >> 4
        vals = E2M1[nib]
    vals = vals * np.repeat(np.exp2(scales.astype(np.float64) - 127.0), 8, axis=1)[..., None]
    return vals.transpose(0, 1, 3, 2).reshape(g * 512, n)


def silu(f):
    return f / (1.0 + np.exp(-np.maximum(f, -700.0)))


def sigm(f):
    return 1.0 / (1.0 + np.exp(-np.maximum(f, -700.0)))


K, N, T = 512, 1024, 1536


def setup_inputs():
    n = np.random.standard_normal
    s = mx_kscale(K)[:, None]
    p_wh = pack_weight(n((K, N)) / np.sqrt(K) / s, "e4m3")
    return {
        "x": (n((K, T)) * s).astype(np.float32),
        "wg": (n((K, N)) / np.sqrt(K) / s).astype(np.float32),
        "wh_words": p_wh[0],
        "wh_scales": p_wh[1],
        "bg": (0.3 * n(N) - 1.0).astype(np.float32),
        "res": (n((N, T))).astype(np.float32),
    }


def reference(x, wg, wh_words, wh_scales, bg, res):
    x_ = mxq(f64(x), 0, "e4m3")
    wg_ = mxq(f64(wg), 0, "e4m3")
    wh_ = unpack_weight(wh_words, wh_scales, "e4m3")
    ga = wg_.T @ x_
    gate = sigm(ga + f64(bg)[:, None])
    ha = wh_.T @ x_
    return f64(res) + gate * (silu(ha) - f64(res))

@@ -1,0 +1,263 @@
+from contextlib import ExitStack
+
+import concourse.mybir as mybir
+from concourse.masks import make_identity
+
+K, N, T = 512, 1024, 1536
+FLOPS = 2 * 2 * K * N * T
+
+F32 = mybir.dt.float32
+BF16 = mybir.dt.bfloat16
+I32 = mybir.dt.int32
+U32 = mybir.dt.uint32
+U8 = mybir.dt.uint8
+FP8X4 = mybir.dt.float8_e4m3fn_x4
+ACT = mybir.ActivationFunctionType
+ALU = mybir.AluOpType
+
+P = 128
+PACK = 4
+CHUNK = 512
+HALF = CHUNK // 2
+BLOCKS = N // P
+CHUNKS = T // CHUNK
+FIRST_GROUPS = ((0, 1), (1, 2), (2, 4), (4, 6), (6, 8))
+PAIRS = ((0, 2), (2, 4), (4, 6), (6, 8))
+
+
+def interleave(copy, raw, grouped):
+    copy(
+        out=grouped.rearrange("p (c i) j -> p c j i", i=4),
+        in_=raw.rearrange("p j (c i) -> p c j i", i=4),
+    )
+
+
+def tile_mix_hway_silu_none_kernel(tc, x, wg, wh_words, wh_scales, bg, res, out):
+    nc = tc.nc
+    x_rows = x.rearrange("(p j) t -> p j t", j=PACK)
+    wg_rows = wg.rearrange("(p j) n -> p j n", j=PACK)
+    wh_flat = wh_words[0].rearrange("p n i -> p (n i)")
+    res_blocks = res.rearrange("(b p) t -> p b t", p=P)
+    out_blocks = out.rearrange("(b p) t -> p b t", p=P)
+
+    units = []
+    for c in range(CHUNKS):
+        for b in range(BLOCKS):
+            if (c, b) in ((0, 0), (CHUNKS - 1, BLOCKS - 1)):
+                units.append((b, c * CHUNK, HALF))
+                units.append((b, c * CHUNK + HALF, HALF))
+            else:
+                units.append((b, c * CHUNK, CHUNK))
+
+    with ExitStack() as ctx:
+        keep = ctx.enter_context(tc.tile_pool(name="keep", bufs=1))
+        work = ctx.enter_context(tc.tile_pool(name="work", bufs=4))
+        psum = ctx.enter_context(tc.psum_pool(name="psum", bufs=3))
+        ctx.enter_context(tc.manual_schedule())
+
+        x_codes = keep.tile([P, T], U32, align_bytes=64)
+        x_scales = keep.tile([P, T], U8, align_bytes=64)
+        wg_codes = keep.tile([P, N], U32, align_bytes=64)
+        wg_scales = keep.tile([P, N], U8, align_bytes=64)
+        wh_codes = keep.tile([P, N], U32, align_bytes=64)
+        wh_plane = keep.tile([P, N], U8, align_bytes=64)
+        bias = keep.tile([P, BLOCKS], F32)
+        half_bias = keep.tile([P, BLOCKS], F32)
+        zero_in = keep.tile([P, 1], F32)
+        zero = keep.tile([P, 1], F32)
+        ident = keep.tile([P, P], F32)
+        stream = [keep.tile([P, BLOCKS, CHUNK], F32, name="stream%d" % c) for c in range(CHUNKS)]
+        x_raw = {}
+        wg_raw = {}
+        x_grouped = [keep.tile([P, HALF, PACK], BF16, name="xg%d" % h, align_bytes=64) for h in range(T // HALF)]
+        wg_grouped = [keep.tile([P, P, PACK], BF16, name="wgg%d" % b, align_bytes=64) for b in range(BLOCKS)]
+
+        def load_x(t0, width):
+            raw = keep.tile([P, PACK, width], F32, name="xraw%d" % t0)
+            nc.sync.dma_start(out=raw[:], in_=x_rows[:, :, t0 : t0 + width])
+            for h in range(width // HALF):
+                x_raw[t0 // HALF + h] = raw[:, :, h * HALF : (h + 1) * HALF]
+
+        def load_wg(b0, b1):
+            raw = keep.tile([P, PACK, (b1 - b0) * P], F32, name="wgraw%d" % b0)
+            nc.sync.dma_start(out=raw[:], in_=wg_rows[:, :, b0 * P : b1 * P])
+            for b in range(b0, b1):
+                wg_raw[b] = raw[:, :, (b - b0) * P : (b - b0 + 1) * P]
+
+        def load_wh(b0, b1):
+            nc.sync.dma_start(
+                out=wh_codes[:, b0 * P : b1 * P].bitcast(I32),
+                in_=wh_flat[:, b0 * P * PACK : b1 * P * PACK].bitcast(I32),
+            )
+
+        def load_res(c, b0, b1):
+            nc.sync.dma_start(out=stream[c][:, b0:b1, :], in_=res_blocks[:, b0:b1, c * CHUNK : (c + 1) * CHUNK])
+
+        nc.vector.memset(wh_plane[:].bitcast(I32), 0)
+        nc.vector.memset(zero_in[:], 0.0)
+        with nc.allow_non_contiguous_dma(reason="one bias value to a partition"):
+            nc.gpsimd.dma_start(out=bias[:], in_=bg.rearrange("(b p) -> p b", p=P))
+        nc.gpsimd.tensor_scalar(out=half_bias[:], in0=bias[:], scalar1=0.5, scalar2=0.0, op0=ALU.mult, op1=ALU.add)
+        make_identity(nc, ident[:])
+
+        load_x(0, HALF)
+        load_wh(0, 1)
+        load_wg(0, 1)
+        for q in range(4):
+            nc.scalar.dma_start(
+                out=wh_plane[32 * q : 32 * q + 4, :].bitcast(I32),
+                in_=wh_scales[0, 4 * q : 4 * q + 4, :].bitcast(I32),
+            )
+        nc.scalar.activation(out=zero[:], in_=zero_in[:], func=ACT.Silu)
+        load_x(HALF, HALF)
+        load_res(0, 0, 1)
+        for b0, b1 in FIRST_GROUPS[1:]:
+            load_wh(b0, b1)
+            load_wg(b0, b1)
+            load_res(0, b0, b1)
+            if b1 == 6:
+                load_x(CHUNK, CHUNK)
+        for c in range(1, CHUNKS):
+            for b0, b1 in PAIRS:
+                load_res(c, b0, b1)
+                if c + 1 < CHUNKS and b0 == 0:
+                    load_x((c + 1) * CHUNK, CHUNK)
+
+        def round_x(h, copy):
+            interleave(copy, x_raw[h], x_grouped[h][:])
+
+        def quantize_x(h):
+            cols = slice(h * HALF, (h + 1) * HALF)
+            nc.vector.quantize_mx(
+                out=x_codes[:, cols].bitcast(FP8X4),
+                scales=x_scales[:, cols],
+                in_=x_grouped[h][:].rearrange("p w j -> p (w j)"),
+            )
+
+        def round_wg(b):
+            interleave(nc.scalar.copy, wg_raw[b], wg_grouped[b][:])
+
+        def quantize_wg(b):
+            cols = slice(b * P, (b + 1) * P)
+            nc.vector.quantize_mx(
+                out=wg_codes[:, cols].bitcast(FP8X4),
+                scales=wg_scales[:, cols],
+                in_=wg_grouped[b][:].rearrange("p w j -> p (w j)"),
+            )
+
+        def product(acc, lhs, rhs):
+            nc.tensor.matmul_mx(
+                out=acc,
+                lhsT=lhs[0].bitcast(FP8X4),
+                lhsT_scale=lhs[1],
+                rhs=rhs[0].bitcast(FP8X4),
+                rhs_scale=rhs[1],
+                start=True,
+                stop=True,
+            )
+
+        def columns(codes, scales, first, width):
+            return codes[:, first : first + width], scales[:, first : first + width]
+
+        def carried(u):
+            b, t0, width = units[u]
+            return stream[t0 // CHUNK][:, b, t0 % CHUNK : t0 % CHUNK + width]
+
+        value = {}
+        turned = {}
+        diff = {}
+        gate = {}
+
+        def value_branch(u):
+            b, t0, width = units[u]
+            ha = psum.tile([P, CHUNK], F32, name="ha")
+            weights = columns(wh_codes, wh_plane, b * P, P)
+            if width == HALF:
+                product(ha[:, :width], weights, columns(x_codes, x_scales, t0, width))
+            else:
+                product(ha[:, :P], weights, columns(x_codes, x_scales, t0, P))
+                for first in range(P, width, P):
+                    product(ha[:, first : first + P], columns(x_codes, x_scales, t0 + first, P), weights)
+            new = work.tile([P, CHUNK], F32, name="new")
+            nc.scalar.activation(out=new[:, :width], in_=ha[:, :width], func=ACT.Silu, bias=zero[:])
+            value[u] = new
+
+        def gate_branch(u):
+            b, t0, width = units[u]
+            ga = psum.tile([P, CHUNK], F32, name="ga")
+            product(ga[:, :width], columns(wg_codes, wg_scales, b * P, P), columns(x_codes, x_scales, t0, width))
+            th = work.tile([P, CHUNK], F32, name="th")
+            nc.scalar.activation(
+                out=th[:, :width], in_=ga[:, :width], func=ACT.Tanh, bias=half_bias[:, b : b + 1], scale=0.5
+            )
+            gate[u] = th[:, :width]
+
+        def turn(u):
+            if units[u][2] == CHUNK:
+                back = psum.tile([P, CHUNK], F32, name="back", bufs=2)
+                for first in range(P, CHUNK, P):
+                    nc.tensor.transpose(back[:, first : first + P], value[u][:, first : first + P], ident[:])
+                turned[u] = back
+
+        def subtract(u):
+            width = units[u][2]
+            gap = work.tile([P, CHUNK], F32, name="gap", bufs=2)
+            if width == HALF:
+                nc.vector.tensor_tensor(out=gap[:, :width], in0=value[u][:, :width], in1=carried(u), op=ALU.subtract)
+            else:
+                nc.gpsimd.tensor_tensor(out=gap[:, :P], in0=value[u][:, :P], in1=carried(u)[:, :P], op=ALU.subtract)
+                nc.vector.tensor_tensor(out=gap[:, P:], in0=turned[u][:, P:], in1=carried(u)[:, P:], op=ALU.subtract)
+            diff[u] = gap[:, :width]
+
+        def weigh(u):
+            nc.vector.scalar_tensor_tensor(
+                out=diff[u], in0=gate[u], scalar=1.0, in1=diff[u], op0=ALU.add, op1=ALU.mult
+            )
+
+        def blend(u):
+            nc.vector.scalar_tensor_tensor(
+                out=carried(u), in0=diff[u], scalar=0.5, in1=carried(u), op0=ALU.mult, op1=ALU.add
+            )
+
+        def store(u):
+            b, t0, width = units[u]
+            c = t0 // CHUNK
+            if c == CHUNKS - 1 and b >= BLOCKS - 2:
+                nc.sync.dma_start(out=out_blocks[:, b, t0 : t0 + width], in_=carried(u))
+            elif b % 2 == 1:
+                nc.sync.dma_start(
+                    out=out_blocks[:, b - 1 : b + 1, c * CHUNK : (c + 1) * CHUNK], in_=stream[c][:, b - 1 : b + 1, :]
+                )
+
+        round_x(0, nc.vector.tensor_copy)
+        round_wg(0)
+        quantize_x(0)
+        round_x(1, nc.vector.tensor_copy)
+        quantize_wg(0)
+        quantize_x(1)
+
+        x_on_scalar = {5: 2, 7: 3, 11: 4, 13: 5}
+        x_quant = {6: 2, 8: 3, 12: 4, 14: 5}
+
+        count = len(units)
+        for s in range(count + 2):
+            if s < count:
+                value_branch(s)
+            if 1 <= s <= count:
+                gate_branch(s - 1)
+                turn(s - 1)
+            if 1 <= s < BLOCKS:
+                round_wg(s)
+            if s in x_on_scalar:
+                round_x(x_on_scalar[s], nc.scalar.copy)
+            if s >= 2:
+                weigh(s - 2)
+            if 1 <= s <= count:
+                subtract(s - 1)
+            if s in x_quant:
+                quantize_x(x_quant[s])
+            if 2 <= s <= BLOCKS:
+                quantize_wg(s - 1)
+            if s >= 2:
+                blend(s - 2)
+                store(s - 2)

@@ -27,8 +27,8 @@ PAIRS = ((0, 2), (2, 4), (4, 6), (6, 8))
 
 def interleave(copy, raw, grouped):
     copy(
-        out=grouped.rearrange("p (c i) j -> p c j i", i=4),
-        in_=raw.rearrange("p j (c i) -> p c j i", i=4),
+        out=grouped.rearrange("p (c i) j -> p c j i", i=2),
+        in_=raw.rearrange("p j (c i) -> p c j i", i=2),
     )
 
 
@@ -61,7 +61,7 @@ def tile_mix_hway_silu_none_kernel(tc, x, wg, wh_words, wh_scales, bg, res, out)
         wg_scales = keep.tile([P, N], U8, align_bytes=64)
         wh_codes = keep.tile([P, N], U32, align_bytes=64)
         wh_plane = keep.tile([P, N], U8, align_bytes=64)
-        bias = keep.tile([P, BLOCKS], F32)
+        bias_rows = keep.tile([P, P], F32)
         half_bias = keep.tile([P, BLOCKS], F32)
         zero_in = keep.tile([P, 1], F32)
         zero = keep.tile([P, 1], F32)
@@ -93,11 +93,10 @@ def tile_mix_hway_silu_none_kernel(tc, x, wg, wh_words, wh_scales, bg, res, out)
         def load_res(c, b0, b1):
             nc.sync.dma_start(out=stream[c][:, b0:b1, :], in_=res_blocks[:, b0:b1, c * CHUNK : (c + 1) * CHUNK])
 
+        nc.vector.memset(bias_rows[:], 0.0)
         nc.vector.memset(wh_plane[:].bitcast(I32), 0)
         nc.vector.memset(zero_in[:], 0.0)
-        with nc.allow_non_contiguous_dma(reason="one bias value to a partition"):
-            nc.gpsimd.dma_start(out=bias[:], in_=bg.rearrange("(b p) -> p b", p=P))
-        nc.gpsimd.tensor_scalar(out=half_bias[:], in0=bias[:], scalar1=0.5, scalar2=0.0, op0=ALU.mult, op1=ALU.add)
+        nc.gpsimd.dma_start(out=bias_rows[:BLOCKS, :], in_=bg.rearrange("(b p) -> b p", p=P))
         make_identity(nc, ident[:])
 
         load_x(0, HALF)
@@ -192,6 +191,11 @@ def tile_mix_hway_silu_none_kernel(tc, x, wg, wh_words, wh_scales, bg, res, out)
             )
             gate[u] = th[:, :width]
 
+        def spread_bias():
+            bias_cols = psum.tile([P, CHUNK], F32, name="back", bufs=2)
+            nc.tensor.transpose(bias_cols[:, :P], bias_rows[:], ident[:])
+            nc.scalar.activation(out=half_bias[:], in_=bias_cols[:, :BLOCKS], func=ACT.Copy, scale=0.5)
+
         def turn(u):
             if units[u][2] == CHUNK:
                 back = psum.tile([P, CHUNK], F32, name="back", bufs=2)
@@ -236,13 +240,16 @@ def tile_mix_hway_silu_none_kernel(tc, x, wg, wh_words, wh_scales, bg, res, out)
         quantize_wg(0)
         quantize_x(1)
 
-        x_on_scalar = {5: 2, 7: 3, 11: 4, 13: 5}
-        x_quant = {6: 2, 8: 3, 12: 4, 14: 5}
+        x_on_scalar = {11: 4, 13: 5}
+        x_on_vector = {6: 2, 7: 3}
+        x_quant = {7: 2, 8: 3, 12: 4, 14: 5}
 
         count = len(units)
         for s in range(count + 2):
             if s < count:
                 value_branch(s)
+            if s == 0:
+                spread_bias()
             if 1 <= s <= count:
                 gate_branch(s - 1)
                 turn(s - 1)
@@ -258,6 +265,8 @@ def tile_mix_hway_silu_none_kernel(tc, x, wg, wh_words, wh_scales, bg, res, out)
                 quantize_x(x_quant[s])
             if 2 <= s <= BLOCKS:
                 quantize_wg(s - 1)
+            if s in x_on_vector:
+                round_x(x_on_vector[s], nc.vector.tensor_copy)
             if s >= 2:
                 blend(s - 2)
                 store(s - 2)

@@ -21,8 +21,10 @@ CHUNK = 512
 HALF = CHUNK // 2
 BLOCKS = N // P
 CHUNKS = T // CHUNK
-FIRST_GROUPS = ((0, 1), (1, 2), (2, 4), (4, 6), (6, 8))
-PAIRS = ((0, 2), (2, 4), (4, 6), (6, 8))
+QUADRANT = 32
+SCALE_ROWS = 4
+PAIRS = tuple((b, b + 2) for b in range(0, BLOCKS, 2))
+FIRST_GROUPS = ((0, 1), (1, 2)) + PAIRS[1:]
 
 
 def interleave(copy, raw, grouped):
@@ -40,14 +42,8 @@ def tile_mix_hway_silu_none_kernel(tc, x, wg, wh_words, wh_scales, bg, res, out)
     res_blocks = res.rearrange("(b p) t -> p b t", p=P)
     out_blocks = out.rearrange("(b p) t -> p b t", p=P)
 
-    units = []
-    for c in range(CHUNKS):
-        for b in range(BLOCKS):
-            if (c, b) in ((0, 0), (CHUNKS - 1, BLOCKS - 1)):
-                units.append((b, c * CHUNK, HALF))
-                units.append((b, c * CHUNK + HALF, HALF))
-            else:
-                units.append((b, c * CHUNK, CHUNK))
+    groups = [(0, b0, b1) for b0, b1 in FIRST_GROUPS[1:]]
+    groups.extend((c, b0, b1) for c in range(1, CHUNKS) for b0, b1 in PAIRS)
 
     with ExitStack() as ctx:
         keep = ctx.enter_context(tc.tile_pool(name="keep", bufs=1))
@@ -70,7 +66,9 @@ def tile_mix_hway_silu_none_kernel(tc, x, wg, wh_words, wh_scales, bg, res, out)
         x_raw = {}
         wg_raw = {}
         x_grouped = [keep.tile([P, HALF, PACK], BF16, name="xg%d" % h, align_bytes=64) for h in range(T // HALF)]
-        wg_grouped = [keep.tile([P, P, PACK], BF16, name="wgg%d" % b, align_bytes=64) for b in range(BLOCKS)]
+        wg_grouped = {
+            b0: keep.tile([P, (b1 - b0) * P, PACK], BF16, name="wgg%d" % b0, align_bytes=64) for b0, b1 in FIRST_GROUPS
+        }
 
         def load_x(t0, width):
             raw = keep.tile([P, PACK, width], F32, name="xraw%d" % t0)
@@ -81,8 +79,7 @@ def tile_mix_hway_silu_none_kernel(tc, x, wg, wh_words, wh_scales, bg, res, out)
         def load_wg(b0, b1):
             raw = keep.tile([P, PACK, (b1 - b0) * P], F32, name="wgraw%d" % b0)
             nc.sync.dma_start(out=raw[:], in_=wg_rows[:, :, b0 * P : b1 * P])
-            for b in range(b0, b1):
-                wg_raw[b] = raw[:, :, (b - b0) * P : (b - b0 + 1) * P]
+            wg_raw[b0] = raw
 
         def load_wh(b0, b1):
             nc.sync.dma_start(
@@ -93,56 +90,61 @@ def tile_mix_hway_silu_none_kernel(tc, x, wg, wh_words, wh_scales, bg, res, out)
         def load_res(c, b0, b1):
             nc.sync.dma_start(out=stream[c][:, b0:b1, :], in_=res_blocks[:, b0:b1, c * CHUNK : (c + 1) * CHUNK])
 
-        nc.vector.memset(bias_rows[:], 0.0)
-        nc.vector.memset(wh_plane[:].bitcast(I32), 0)
+        def store(c, b0, b1):
+            nc.sync.dma_start(out=out_blocks[:, b0:b1, c * CHUNK : (c + 1) * CHUNK], in_=stream[c][:, b0:b1, :])
+
+        nc.gpsimd.memset(wh_plane[:].bitcast(I32), 0)
+        nc.gpsimd.memset(bias_rows[:], 0.0)
         nc.vector.memset(zero_in[:], 0.0)
         nc.gpsimd.dma_start(out=bias_rows[:BLOCKS, :], in_=bg.rearrange("(b p) -> b p", p=P))
         make_identity(nc, ident[:])
 
         load_x(0, HALF)
-        load_wh(0, 1)
-        load_wg(0, 1)
-        for q in range(4):
-            nc.scalar.dma_start(
-                out=wh_plane[32 * q : 32 * q + 4, :].bitcast(I32),
-                in_=wh_scales[0, 4 * q : 4 * q + 4, :].bitcast(I32),
+        for q in range(P // QUADRANT):
+            nc.sync.dma_start(
+                out=wh_plane[QUADRANT * q : QUADRANT * q + SCALE_ROWS, :].bitcast(I32),
+                in_=wh_scales[0, SCALE_ROWS * q : SCALE_ROWS * (q + 1), :].bitcast(I32),
             )
         nc.scalar.activation(out=zero[:], in_=zero_in[:], func=ACT.Silu)
+        load_wh(*FIRST_GROUPS[0])
+        load_wg(*FIRST_GROUPS[0])
         load_x(HALF, HALF)
-        load_res(0, 0, 1)
-        for b0, b1 in FIRST_GROUPS[1:]:
-            load_wh(b0, b1)
-            load_wg(b0, b1)
-            load_res(0, b0, b1)
-            if b1 == 6:
+        load_res(0, *FIRST_GROUPS[0])
+        load_wg(*FIRST_GROUPS[1])
+        load_wh(*FIRST_GROUPS[1])
+        for this, following in zip(FIRST_GROUPS[1:], FIRST_GROUPS[2:]):
+            load_wg(*following)
+            load_res(0, *this)
+            if following == FIRST_GROUPS[-1]:
                 load_x(CHUNK, CHUNK)
+            load_wh(*following)
+        load_res(0, *FIRST_GROUPS[-1])
         for c in range(1, CHUNKS):
-            for b0, b1 in PAIRS:
-                load_res(c, b0, b1)
-                if c + 1 < CHUNKS and b0 == 0:
-                    load_x((c + 1) * CHUNK, CHUNK)
+            load_res(c, *PAIRS[0])
+            if c + 1 < CHUNKS:
+                load_x((c + 1) * CHUNK, CHUNK)
+            for pair in PAIRS[1:]:
+                load_res(c, *pair)
 
         def round_x(h, copy):
             interleave(copy, x_raw[h], x_grouped[h][:])
 
+        def round_wg(b0):
+            interleave(nc.scalar.copy, wg_raw[b0][:], wg_grouped[b0][:])
+
+        def quantize(codes, scales, first, grouped):
+            cols = slice(first, first + grouped.shape[1])
+            nc.vector.quantize_mx(
+                out=codes[:, cols].bitcast(FP8X4),
+                scales=scales[:, cols],
+                in_=grouped[:].rearrange("p w j -> p (w j)"),
+            )
+
         def quantize_x(h):
-            cols = slice(h * HALF, (h + 1) * HALF)
-            nc.vector.quantize_mx(
-                out=x_codes[:, cols].bitcast(FP8X4),
-                scales=x_scales[:, cols],
-                in_=x_grouped[h][:].rearrange("p w j -> p (w j)"),
-            )
+            quantize(x_codes, x_scales, h * HALF, x_grouped[h])
 
-        def round_wg(b):
-            interleave(nc.scalar.copy, wg_raw[b], wg_grouped[b][:])
-
-        def quantize_wg(b):
-            cols = slice(b * P, (b + 1) * P)
-            nc.vector.quantize_mx(
-                out=wg_codes[:, cols].bitcast(FP8X4),
-                scales=wg_scales[:, cols],
-                in_=wg_grouped[b][:].rearrange("p w j -> p (w j)"),
-            )
+        def quantize_wg(b0):
+            quantize(wg_codes, wg_scales, b0 * P, wg_grouped[b0])
 
         def product(acc, lhs, rhs):
             nc.tensor.matmul_mx(
@@ -158,115 +160,121 @@ def tile_mix_hway_silu_none_kernel(tc, x, wg, wh_words, wh_scales, bg, res, out)
         def columns(codes, scales, first, width):
             return codes[:, first : first + width], scales[:, first : first + width]
 
-        def carried(u):
-            b, t0, width = units[u]
-            return stream[t0 // CHUNK][:, b, t0 % CHUNK : t0 % CHUNK + width]
-
-        value = {}
-        turned = {}
-        diff = {}
-        gate = {}
-
-        def value_branch(u):
-            b, t0, width = units[u]
+        def value_branch(b, t0, width, upright):
             ha = psum.tile([P, CHUNK], F32, name="ha")
             weights = columns(wh_codes, wh_plane, b * P, P)
-            if width == HALF:
-                product(ha[:, :width], weights, columns(x_codes, x_scales, t0, width))
-            else:
-                product(ha[:, :P], weights, columns(x_codes, x_scales, t0, P))
-                for first in range(P, width, P):
-                    product(ha[:, first : first + P], columns(x_codes, x_scales, t0 + first, P), weights)
-            new = work.tile([P, CHUNK], F32, name="new")
-            nc.scalar.activation(out=new[:, :width], in_=ha[:, :width], func=ACT.Silu, bias=zero[:])
-            value[u] = new
+            if upright:
+                product(ha[:, :upright], weights, columns(x_codes, x_scales, t0, upright))
+            for first in range(upright, width, P):
+                product(ha[:, first : first + P], columns(x_codes, x_scales, t0 + first, P), weights)
+            value = work.tile([P, CHUNK], F32, name="value")
+            nc.scalar.activation(out=value[:, :width], in_=ha[:, :width], func=ACT.Silu, bias=zero[:])
+            return value
 
-        def gate_branch(u):
-            b, t0, width = units[u]
+        def gate_branch(b, t0, width, tanh_out):
             ga = psum.tile([P, CHUNK], F32, name="ga")
             product(ga[:, :width], columns(wg_codes, wg_scales, b * P, P), columns(x_codes, x_scales, t0, width))
-            th = work.tile([P, CHUNK], F32, name="th")
             nc.scalar.activation(
-                out=th[:, :width], in_=ga[:, :width], func=ACT.Tanh, bias=half_bias[:, b : b + 1], scale=0.5
+                out=tanh_out, in_=ga[:, :width], func=ACT.Tanh, bias=half_bias[:, b : b + 1], scale=0.5
             )
-            gate[u] = th[:, :width]
 
         def spread_bias():
             bias_cols = psum.tile([P, CHUNK], F32, name="back", bufs=2)
             nc.tensor.transpose(bias_cols[:, :P], bias_rows[:], ident[:])
             nc.scalar.activation(out=half_bias[:], in_=bias_cols[:, :BLOCKS], func=ACT.Copy, scale=0.5)
 
-        def turn(u):
-            if units[u][2] == CHUNK:
-                back = psum.tile([P, CHUNK], F32, name="back", bufs=2)
-                for first in range(P, CHUNK, P):
-                    nc.tensor.transpose(back[:, first : first + P], value[u][:, first : first + P], ident[:])
-                turned[u] = back
+        def turn(value, upright):
+            back = psum.tile([P, CHUNK], F32, name="back", bufs=2)
+            for first in range(upright, CHUNK, P):
+                nc.tensor.transpose(back[:, first : first + P], value[:, first : first + P], ident[:])
+            return back
 
-        def subtract(u):
-            width = units[u][2]
-            gap = work.tile([P, CHUNK], F32, name="gap", bufs=2)
-            if width == HALF:
-                nc.vector.tensor_tensor(out=gap[:, :width], in0=value[u][:, :width], in1=carried(u), op=ALU.subtract)
-            else:
-                nc.gpsimd.tensor_tensor(out=gap[:, :P], in0=value[u][:, :P], in1=carried(u)[:, :P], op=ALU.subtract)
-                nc.vector.tensor_tensor(out=gap[:, P:], in0=turned[u][:, P:], in1=carried(u)[:, P:], op=ALU.subtract)
-            diff[u] = gap[:, :width]
+        def subtract(engine, gap, value, carried):
+            engine.tensor_tensor(out=gap, in0=value, in1=carried, op=ALU.subtract)
 
-        def weigh(u):
-            nc.vector.scalar_tensor_tensor(
-                out=diff[u], in0=gate[u], scalar=1.0, in1=diff[u], op0=ALU.add, op1=ALU.mult
-            )
+        def weigh(gap, tanh):
+            nc.vector.scalar_tensor_tensor(out=gap, in0=tanh, scalar=1.0, in1=gap, op0=ALU.add, op1=ALU.mult)
 
-        def blend(u):
-            nc.vector.scalar_tensor_tensor(
-                out=carried(u), in0=diff[u], scalar=0.5, in1=carried(u), op0=ALU.mult, op1=ALU.add
-            )
+        def blend(carried, gap):
+            nc.vector.scalar_tensor_tensor(out=carried, in0=gap, scalar=0.5, in1=carried, op0=ALU.mult, op1=ALU.add)
 
-        def store(u):
-            b, t0, width = units[u]
-            c = t0 // CHUNK
-            if c == CHUNKS - 1 and b >= BLOCKS - 2:
-                nc.sync.dma_start(out=out_blocks[:, b, t0 : t0 + width], in_=carried(u))
-            elif b % 2 == 1:
-                nc.sync.dma_start(
-                    out=out_blocks[:, b - 1 : b + 1, c * CHUNK : (c + 1) * CHUNK], in_=stream[c][:, b - 1 : b + 1, :]
-                )
+        def tanh_tile():
+            return work.tile([P, 2 * CHUNK], F32, name="tanh", bufs=3)
 
+        def gap_tile():
+            return work.tile([P, 2 * CHUNK], F32, name="gap", bufs=2)
+
+        tanh, gap = tanh_tile(), gap_tile()
+        lower, upper = slice(0, HALF), slice(HALF, CHUNK)
+        carried = stream[0][:, 0, :]
         round_x(0, nc.vector.tensor_copy)
         round_wg(0)
         quantize_x(0)
-        round_x(1, nc.vector.tensor_copy)
+        value = value_branch(0, 0, HALF, HALF)
         quantize_wg(0)
+        spread_bias()
+        gate_branch(0, 0, HALF, tanh[:, lower])
+        round_x(1, nc.vector.tensor_copy)
+        subtract(nc.vector, gap[:, lower], value[:, :HALF], carried[:, lower])
         quantize_x(1)
+        round_wg(1)
+        value = value_branch(0, HALF, HALF, HALF)
+        gate_branch(0, HALF, HALF, tanh[:, upper])
+        weigh(gap[:, lower], tanh[:, lower])
+        quantize_wg(1)
+        blend(carried[:, lower], gap[:, lower])
+        subtract(nc.vector, gap[:, upper], value[:, :HALF], carried[:, upper])
+        last_carried, last_gap, last_tanh = carried[:, upper], gap[:, upper], tanh[:, upper]
 
-        x_on_scalar = {11: 4, 13: 5}
-        x_on_vector = {6: 2, 7: 3}
-        x_quant = {7: 2, 8: 3, 12: 4, 14: 5}
+        chunk1_start = len(FIRST_GROUPS) - 1
+        chunk1_round = chunk1_start - 2
+        chunk1_halves = (2, 3)
+        chunk2_halves = (4, 5)
 
-        count = len(units)
-        for s in range(count + 2):
-            if s < count:
-                value_branch(s)
-            if s == 0:
-                spread_bias()
-            if 1 <= s <= count:
-                gate_branch(s - 1)
-                turn(s - 1)
-            if 1 <= s < BLOCKS:
-                round_wg(s)
-            if s in x_on_scalar:
-                round_x(x_on_scalar[s], nc.scalar.copy)
-            if s >= 2:
-                weigh(s - 2)
-            if 1 <= s <= count:
-                subtract(s - 1)
-            if s in x_quant:
-                quantize_x(x_quant[s])
-            if 2 <= s <= BLOCKS:
-                quantize_wg(s - 1)
-            if s in x_on_vector:
-                round_x(x_on_vector[s], nc.vector.tensor_copy)
-            if s >= 2:
-                blend(s - 2)
-                store(s - 2)
+        for g, (c, b0, b1) in enumerate(groups):
+            t0 = c * CHUNK
+            blocks = range(b0, b1)
+            share = len(blocks) * CHUNK // 4
+            upright_of = {b: share if b == b0 else 0 for b in blocks}
+            next_wg = b1 if c == 0 and b1 < BLOCKS else None
+
+            values = {b: value_branch(b, t0, CHUNK, upright_of[b]) for b in blocks}
+            if next_wg:
+                round_wg(next_wg)
+            if 0 <= g - chunk1_start < len(chunk2_halves):
+                round_x(chunk2_halves[g - chunk1_start], nc.scalar.copy)
+            tanh = tanh_tile()
+            for b in blocks:
+                gate_branch(b, t0, CHUNK, tanh[:, (b - b0) * CHUNK : (b - b0 + 1) * CHUNK])
+            backs = {b: turn(values[b], upright_of[b]) for b in blocks}
+
+            weigh(last_gap, last_tanh)
+            gap = gap_tile()
+            carried = stream[c][:, b0:b1, :].rearrange("p b t -> p (b t)")
+            subtract(nc.gpsimd, gap[:, :share], values[b0][:, :share], carried[:, :share])
+            for b in blocks:
+                cols = slice((b - b0) * CHUNK + upright_of[b], (b - b0 + 1) * CHUNK)
+                subtract(nc.vector, gap[:, cols], backs[b][:, upright_of[b] :], carried[:, cols])
+            if g == chunk1_round:
+                for h in chunk1_halves:
+                    round_x(h, nc.vector.tensor_copy)
+                for h in chunk1_halves:
+                    quantize_x(h)
+            if 0 <= g - chunk1_start - 1 < len(chunk2_halves):
+                quantize_x(chunk2_halves[g - chunk1_start - 1])
+            if next_wg:
+                quantize_wg(next_wg)
+            blend(last_carried, last_gap)
+            if g > 0:
+                last_c, last_b0, last_b1 = groups[g - 1]
+                store(last_c, last_b1 - 2, last_b1)
+            width = len(blocks) * CHUNK
+            last_carried, last_gap, last_tanh = carried, gap[:, :width], tanh[:, :width]
+
+        for cols in (slice(0, CHUNK), slice(CHUNK, 2 * CHUNK)):
+            weigh(last_gap[:, cols], last_tanh[:, cols])
+        for b, first, width in ((0, 0, CHUNK), (1, 0, HALF), (1, HALF, HALF)):
+            cols = slice(b * CHUNK + first, b * CHUNK + first + width)
+            t0 = T - CHUNK + first
+            blend(last_carried[:, cols], last_gap[:, cols])
+            nc.sync.dma_start(out=out_blocks[:, BLOCKS - 2 + b, t0 : t0 + width], in_=last_carried[:, cols])

@@ -47,8 +47,8 @@ def tile_mix_hway_silu_none_kernel(tc, x, wg, wh_words, wh_scales, bg, res, out)
 
     with ExitStack() as ctx:
         keep = ctx.enter_context(tc.tile_pool(name="keep", bufs=1))
-        work = ctx.enter_context(tc.tile_pool(name="work", bufs=4))
-        psum = ctx.enter_context(tc.psum_pool(name="psum", bufs=3))
+        work = ctx.enter_context(tc.tile_pool(name="work", bufs=3))
+        psum = ctx.enter_context(tc.psum_pool(name="psum", bufs=2))
         ctx.enter_context(tc.manual_schedule())
 
         x_codes = keep.tile([P, T], U32, align_bytes=64)
@@ -160,14 +160,14 @@ def tile_mix_hway_silu_none_kernel(tc, x, wg, wh_words, wh_scales, bg, res, out)
         def columns(codes, scales, first, width):
             return codes[:, first : first + width], scales[:, first : first + width]
 
-        def value_branch(b, t0, width, upright):
+        def value_branch(b, t0, width, turned):
             ha = psum.tile([P, CHUNK], F32, name="ha")
             weights = columns(wh_codes, wh_plane, b * P, P)
-            if upright:
-                product(ha[:, :upright], weights, columns(x_codes, x_scales, t0, upright))
-            for first in range(upright, width, P):
+            if turned < width:
+                product(ha[:, turned:width], weights, columns(x_codes, x_scales, t0 + turned, width - turned))
+            for first in range(0, turned, P):
                 product(ha[:, first : first + P], columns(x_codes, x_scales, t0 + first, P), weights)
-            value = work.tile([P, CHUNK], F32, name="value")
+            value = work.tile([P, CHUNK], F32, name="value", bufs=6)
             nc.scalar.activation(out=value[:, :width], in_=ha[:, :width], func=ACT.Silu, bias=zero[:])
             return value
 
@@ -179,27 +179,50 @@ def tile_mix_hway_silu_none_kernel(tc, x, wg, wh_words, wh_scales, bg, res, out)
             )
 
         def spread_bias():
-            bias_cols = psum.tile([P, CHUNK], F32, name="back", bufs=2)
+            bias_cols = psum.tile([P, CHUNK], F32, name="back")
             nc.tensor.transpose(bias_cols[:, :P], bias_rows[:], ident[:])
             nc.scalar.activation(out=half_bias[:], in_=bias_cols[:, :BLOCKS], func=ACT.Copy, scale=0.5)
 
-        def turn(value, upright):
-            back = psum.tile([P, CHUNK], F32, name="back", bufs=2)
-            for first in range(upright, CHUNK, P):
+        def turn_back(value, turned):
+            back = psum.tile([P, CHUNK], F32, name="back")
+            for first in range(0, turned, P):
                 nc.tensor.transpose(back[:, first : first + P], value[:, first : first + P], ident[:])
             return back
+
+        def negate_res(c, b):
+            flipped = psum.tile([P, CHUNK], F32, name="flipped", bufs=1)
+            for first in range(0, HALF, P):
+                nc.tensor.transpose(flipped[:, first : first + P], stream[c][:, b, first : first + P], ident[:])
+            minus_res = work.tile([P, HALF], F32, name="minus_res")
+            nc.scalar.activation(out=minus_res[:], in_=flipped[:, :HALF], func=ACT.Copy, scale=-1.0)
+            return minus_res
+
+        def add_in_psum(value, minus_res):
+            total = psum.tile([P, CHUNK], F32, name="total", bufs=1)
+            for first in range(0, HALF, P):
+                cols = slice(first, first + P)
+                for term, opens in ((value, True), (minus_res, False)):
+                    nc.tensor.matmul(
+                        total[:, cols],
+                        lhsT=term[:, cols],
+                        rhs=ident[:],
+                        is_transpose=True,
+                        start=opens,
+                        stop=not opens,
+                    )
+            return total[:, :HALF]
 
         def subtract(engine, gap, value, carried):
             engine.tensor_tensor(out=gap, in0=value, in1=carried, op=ALU.subtract)
 
-        def weigh(gap, tanh):
-            nc.vector.scalar_tensor_tensor(out=gap, in0=tanh, scalar=1.0, in1=gap, op0=ALU.add, op1=ALU.mult)
+        def weigh(gap, tanh, difference):
+            nc.vector.scalar_tensor_tensor(out=gap, in0=tanh, scalar=1.0, in1=difference, op0=ALU.add, op1=ALU.mult)
 
         def blend(carried, gap):
             nc.vector.scalar_tensor_tensor(out=carried, in0=gap, scalar=0.5, in1=carried, op0=ALU.mult, op1=ALU.add)
 
         def tanh_tile():
-            return work.tile([P, 2 * CHUNK], F32, name="tanh", bufs=3)
+            return work.tile([P, 2 * CHUNK], F32, name="tanh")
 
         def gap_tile():
             return work.tile([P, 2 * CHUNK], F32, name="gap", bufs=2)
@@ -210,7 +233,7 @@ def tile_mix_hway_silu_none_kernel(tc, x, wg, wh_words, wh_scales, bg, res, out)
         round_x(0, nc.vector.tensor_copy)
         round_wg(0)
         quantize_x(0)
-        value = value_branch(0, 0, HALF, HALF)
+        value = value_branch(0, 0, HALF, 0)
         quantize_wg(0)
         spread_bias()
         gate_branch(0, 0, HALF, tanh[:, lower])
@@ -218,9 +241,9 @@ def tile_mix_hway_silu_none_kernel(tc, x, wg, wh_words, wh_scales, bg, res, out)
         subtract(nc.vector, gap[:, lower], value[:, :HALF], carried[:, lower])
         quantize_x(1)
         round_wg(1)
-        value = value_branch(0, HALF, HALF, HALF)
+        value = value_branch(0, HALF, HALF, 0)
         gate_branch(0, HALF, HALF, tanh[:, upper])
-        weigh(gap[:, lower], tanh[:, lower])
+        weigh(gap[:, lower], tanh[:, lower], gap[:, lower])
         quantize_wg(1)
         blend(carried[:, lower], gap[:, lower])
         subtract(nc.vector, gap[:, upper], value[:, :HALF], carried[:, upper])
@@ -230,15 +253,19 @@ def tile_mix_hway_silu_none_kernel(tc, x, wg, wh_words, wh_scales, bg, res, out)
         chunk1_round = chunk1_start - 2
         chunk1_halves = (2, 3)
         chunk2_halves = (4, 5)
+        summed_from = chunk1_start + len(chunk2_halves)
+        minus_res = None
+        last_terms = None
 
         for g, (c, b0, b1) in enumerate(groups):
             t0 = c * CHUNK
             blocks = range(b0, b1)
-            share = len(blocks) * CHUNK // 4
-            upright_of = {b: share if b == b0 else 0 for b in blocks}
+            upright_from = CHUNK - len(blocks) * CHUNK // 4
+            turned = {b: upright_from if b == b0 else CHUNK for b in blocks}
+            summed = g >= summed_from
             next_wg = b1 if c == 0 and b1 < BLOCKS else None
 
-            values = {b: value_branch(b, t0, CHUNK, upright_of[b]) for b in blocks}
+            values = {b: value_branch(b, t0, CHUNK, turned[b]) for b in blocks}
             if next_wg:
                 round_wg(next_wg)
             if 0 <= g - chunk1_start < len(chunk2_halves):
@@ -246,15 +273,25 @@ def tile_mix_hway_silu_none_kernel(tc, x, wg, wh_words, wh_scales, bg, res, out)
             tanh = tanh_tile()
             for b in blocks:
                 gate_branch(b, t0, CHUNK, tanh[:, (b - b0) * CHUNK : (b - b0 + 1) * CHUNK])
-            backs = {b: turn(values[b], upright_of[b]) for b in blocks}
+            last_total = add_in_psum(*last_terms) if last_terms else None
+            last_terms = (values[b0], minus_res) if summed else None
+            if summed_from <= g + 1 < len(groups):
+                minus_res = negate_res(*groups[g + 1][:2])
+            on_vector = blocks[1:] if summed else blocks
+            backs = {b: turn_back(values[b], turned[b]) for b in on_vector}
 
-            weigh(last_gap, last_tanh)
+            if last_total is None:
+                weigh(last_gap, last_tanh, last_gap)
+            else:
+                weigh(last_gap[:, HALF:], last_tanh[:, HALF:], last_gap[:, HALF:])
+                weigh(last_gap[:, :HALF], last_tanh[:, :HALF], last_total)
             gap = gap_tile()
             carried = stream[c][:, b0:b1, :].rearrange("p b t -> p (b t)")
-            subtract(nc.gpsimd, gap[:, :share], values[b0][:, :share], carried[:, :share])
-            for b in blocks:
-                cols = slice((b - b0) * CHUNK + upright_of[b], (b - b0 + 1) * CHUNK)
-                subtract(nc.vector, gap[:, cols], backs[b][:, upright_of[b] :], carried[:, cols])
+            upright = slice(upright_from, CHUNK)
+            subtract(nc.gpsimd, gap[:, upright], values[b0][:, upright], carried[:, upright])
+            for b in on_vector:
+                cols = slice((b - b0) * CHUNK, (b - b0) * CHUNK + turned[b])
+                subtract(nc.vector, gap[:, cols], backs[b][:, : turned[b]], carried[:, cols])
             if g == chunk1_round:
                 for h in chunk1_halves:
                     round_x(h, nc.vector.tensor_copy)
@@ -271,10 +308,13 @@ def tile_mix_hway_silu_none_kernel(tc, x, wg, wh_words, wh_scales, bg, res, out)
             width = len(blocks) * CHUNK
             last_carried, last_gap, last_tanh = carried, gap[:, :width], tanh[:, :width]
 
-        for cols in (slice(0, CHUNK), slice(CHUNK, 2 * CHUNK)):
-            weigh(last_gap[:, cols], last_tanh[:, cols])
-        for b, first, width in ((0, 0, CHUNK), (1, 0, HALF), (1, HALF, HALF)):
-            cols = slice(b * CHUNK + first, b * CHUNK + first + width)
+        weigh(last_gap[:, :HALF], last_tanh[:, :HALF], add_in_psum(*last_terms))
+        weigh(last_gap[:, HALF:CHUNK], last_tanh[:, HALF:CHUNK], last_gap[:, HALF:CHUNK])
+        pieces = ((0, 0, CHUNK), (1, 0, HALF), (1, HALF, HALF))
+        spans = [slice(b * CHUNK + first, b * CHUNK + first + width) for b, first, width in pieces]
+        for i, (b, first, width) in enumerate(pieces):
+            if i + 1 < len(pieces):
+                weigh(last_gap[:, spans[i + 1]], last_tanh[:, spans[i + 1]], last_gap[:, spans[i + 1]])
+            blend(last_carried[:, spans[i]], last_gap[:, spans[i]])
             t0 = T - CHUNK + first
-            blend(last_carried[:, cols], last_gap[:, cols])
-            nc.sync.dma_start(out=out_blocks[:, BLOCKS - 2 + b, t0 : t0 + width], in_=last_carried[:, cols])
+            nc.sync.dma_start(out=out_blocks[:, BLOCKS - 2 + b, t0 : t0 + width], in_=last_carried[:, spans[i]])

from contextlib import ExitStack

import concourse.mybir as mybir
from concourse.masks import make_identity

K, N, T = 512, 1024, 1536
FLOPS = 2 * 2 * K * N * T

F32 = mybir.dt.float32
BF16 = mybir.dt.bfloat16
I32 = mybir.dt.int32
U32 = mybir.dt.uint32
U8 = mybir.dt.uint8
FP8X4 = mybir.dt.float8_e4m3fn_x4
ACT = mybir.ActivationFunctionType
ALU = mybir.AluOpType

P = 128
PACK = 4
CHUNK = 512
HALF = CHUNK // 2
BLOCKS = N // P
CHUNKS = T // CHUNK
QUADRANT = 32
SCALE_ROWS = 4
PAIRS = tuple((b, b + 2) for b in range(0, BLOCKS, 2))
FIRST_GROUPS = ((0, 1), (1, 2)) + PAIRS[1:]


def interleave(copy, raw, grouped):
    copy(
        out=grouped.rearrange("p (c i) j -> p c j i", i=2),
        in_=raw.rearrange("p j (c i) -> p c j i", i=2),
    )


def tile_mix_hway_silu_none_kernel(tc, x, wg, wh_words, wh_scales, bg, res, out):
    nc = tc.nc
    x_rows = x.rearrange("(p j) t -> p j t", j=PACK)
    wg_rows = wg.rearrange("(p j) n -> p j n", j=PACK)
    wh_flat = wh_words[0].rearrange("p n i -> p (n i)")
    res_blocks = res.rearrange("(b p) t -> p b t", p=P)
    out_blocks = out.rearrange("(b p) t -> p b t", p=P)

    groups = [(0, b0, b1) for b0, b1 in FIRST_GROUPS[1:]]
    groups.extend((c, b0, b1) for c in range(1, CHUNKS) for b0, b1 in PAIRS)

    with ExitStack() as ctx:
        keep = ctx.enter_context(tc.tile_pool(name="keep", bufs=1))
        work = ctx.enter_context(tc.tile_pool(name="work", bufs=3))
        psum = ctx.enter_context(tc.psum_pool(name="psum", bufs=2))
        ctx.enter_context(tc.manual_schedule())

        x_codes = keep.tile([P, T], U32, align_bytes=64)
        x_scales = keep.tile([P, T], U8, align_bytes=64)
        wg_codes = keep.tile([P, N], U32, align_bytes=64)
        wg_scales = keep.tile([P, N], U8, align_bytes=64)
        wh_codes = keep.tile([P, N], U32, align_bytes=64)
        wh_plane = keep.tile([P, N], U8, align_bytes=64)
        bias_rows = keep.tile([P, P], F32)
        half_bias = keep.tile([P, BLOCKS], F32)
        zero_in = keep.tile([P, 1], F32)
        zero = keep.tile([P, 1], F32)
        ident = keep.tile([P, P], F32)
        stream = [keep.tile([P, BLOCKS, CHUNK], F32, name="stream%d" % c) for c in range(CHUNKS)]
        x_raw = {}
        wg_raw = {}
        x_grouped = [keep.tile([P, HALF, PACK], BF16, name="xg%d" % h, align_bytes=64) for h in range(T // HALF)]
        wg_grouped = {
            b0: keep.tile([P, (b1 - b0) * P, PACK], BF16, name="wgg%d" % b0, align_bytes=64) for b0, b1 in FIRST_GROUPS
        }

        def load_x(t0, width):
            raw = keep.tile([P, PACK, width], F32, name="xraw%d" % t0)
            nc.sync.dma_start(out=raw[:], in_=x_rows[:, :, t0 : t0 + width])
            for h in range(width // HALF):
                x_raw[t0 // HALF + h] = raw[:, :, h * HALF : (h + 1) * HALF]

        def load_wg(b0, b1):
            raw = keep.tile([P, PACK, (b1 - b0) * P], F32, name="wgraw%d" % b0)
            nc.sync.dma_start(out=raw[:], in_=wg_rows[:, :, b0 * P : b1 * P])
            wg_raw[b0] = raw

        def load_wh(b0, b1):
            nc.sync.dma_start(
                out=wh_codes[:, b0 * P : b1 * P].bitcast(I32),
                in_=wh_flat[:, b0 * P * PACK : b1 * P * PACK].bitcast(I32),
            )

        def load_res(c, b0, b1):
            nc.sync.dma_start(out=stream[c][:, b0:b1, :], in_=res_blocks[:, b0:b1, c * CHUNK : (c + 1) * CHUNK])

        def store(c, b0, b1):
            nc.sync.dma_start(out=out_blocks[:, b0:b1, c * CHUNK : (c + 1) * CHUNK], in_=stream[c][:, b0:b1, :])

        nc.gpsimd.memset(wh_plane[:].bitcast(I32), 0)
        nc.gpsimd.memset(bias_rows[:], 0.0)
        nc.vector.memset(zero_in[:], 0.0)
        nc.gpsimd.dma_start(out=bias_rows[:BLOCKS, :], in_=bg.rearrange("(b p) -> b p", p=P))
        make_identity(nc, ident[:])

        load_x(0, HALF)
        for q in range(P // QUADRANT):
            nc.sync.dma_start(
                out=wh_plane[QUADRANT * q : QUADRANT * q + SCALE_ROWS, :].bitcast(I32),
                in_=wh_scales[0, SCALE_ROWS * q : SCALE_ROWS * (q + 1), :].bitcast(I32),
            )
        nc.scalar.activation(out=zero[:], in_=zero_in[:], func=ACT.Silu)
        load_wh(*FIRST_GROUPS[0])
        load_wg(*FIRST_GROUPS[0])
        load_x(HALF, HALF)
        load_res(0, *FIRST_GROUPS[0])
        load_wg(*FIRST_GROUPS[1])
        load_wh(*FIRST_GROUPS[1])
        for this, following in zip(FIRST_GROUPS[1:], FIRST_GROUPS[2:]):
            load_wg(*following)
            load_res(0, *this)
            if following == FIRST_GROUPS[-1]:
                load_x(CHUNK, CHUNK)
            load_wh(*following)
        load_res(0, *FIRST_GROUPS[-1])
        for c in range(1, CHUNKS):
            load_res(c, *PAIRS[0])
            if c + 1 < CHUNKS:
                load_x((c + 1) * CHUNK, CHUNK)
            for pair in PAIRS[1:]:
                load_res(c, *pair)

        def round_x(h, copy):
            interleave(copy, x_raw[h], x_grouped[h][:])

        def round_wg(b0):
            interleave(nc.scalar.copy, wg_raw[b0][:], wg_grouped[b0][:])

        def quantize(codes, scales, first, grouped):
            cols = slice(first, first + grouped.shape[1])
            nc.vector.quantize_mx(
                out=codes[:, cols].bitcast(FP8X4),
                scales=scales[:, cols],
                in_=grouped[:].rearrange("p w j -> p (w j)"),
            )

        def quantize_x(h):
            quantize(x_codes, x_scales, h * HALF, x_grouped[h])

        def quantize_wg(b0):
            quantize(wg_codes, wg_scales, b0 * P, wg_grouped[b0])

        def product(acc, lhs, rhs):
            nc.tensor.matmul_mx(
                out=acc,
                lhsT=lhs[0].bitcast(FP8X4),
                lhsT_scale=lhs[1],
                rhs=rhs[0].bitcast(FP8X4),
                rhs_scale=rhs[1],
                start=True,
                stop=True,
            )

        def columns(codes, scales, first, width):
            return codes[:, first : first + width], scales[:, first : first + width]

        def value_branch(b, t0, width, turned):
            ha = psum.tile([P, CHUNK], F32, name="ha")
            weights = columns(wh_codes, wh_plane, b * P, P)
            if turned < width:
                product(ha[:, turned:width], weights, columns(x_codes, x_scales, t0 + turned, width - turned))
            for first in range(0, turned, P):
                product(ha[:, first : first + P], columns(x_codes, x_scales, t0 + first, P), weights)
            value = work.tile([P, CHUNK], F32, name="value", bufs=6)
            nc.scalar.activation(out=value[:, :width], in_=ha[:, :width], func=ACT.Silu, bias=zero[:])
            return value

        def gate_branch(b, t0, width, tanh_out):
            ga = psum.tile([P, CHUNK], F32, name="ga")
            product(ga[:, :width], columns(wg_codes, wg_scales, b * P, P), columns(x_codes, x_scales, t0, width))
            nc.scalar.activation(
                out=tanh_out, in_=ga[:, :width], func=ACT.Tanh, bias=half_bias[:, b : b + 1], scale=0.5
            )

        def spread_bias():
            bias_cols = psum.tile([P, CHUNK], F32, name="back")
            nc.tensor.transpose(bias_cols[:, :P], bias_rows[:], ident[:])
            nc.scalar.activation(out=half_bias[:], in_=bias_cols[:, :BLOCKS], func=ACT.Copy, scale=0.5)

        def turn_back(value, turned):
            back = psum.tile([P, CHUNK], F32, name="back")
            for first in range(0, turned, P):
                nc.tensor.transpose(back[:, first : first + P], value[:, first : first + P], ident[:])
            return back

        def negate_res(c, b):
            flipped = psum.tile([P, CHUNK], F32, name="flipped", bufs=1)
            for first in range(0, HALF, P):
                nc.tensor.transpose(flipped[:, first : first + P], stream[c][:, b, first : first + P], ident[:])
            minus_res = work.tile([P, HALF], F32, name="minus_res")
            nc.scalar.activation(out=minus_res[:], in_=flipped[:, :HALF], func=ACT.Copy, scale=-1.0)
            return minus_res

        def add_in_psum(value, minus_res):
            total = psum.tile([P, CHUNK], F32, name="total", bufs=1)
            for first in range(0, HALF, P):
                cols = slice(first, first + P)
                for term, opens in ((value, True), (minus_res, False)):
                    nc.tensor.matmul(
                        total[:, cols],
                        lhsT=term[:, cols],
                        rhs=ident[:],
                        is_transpose=True,
                        start=opens,
                        stop=not opens,
                    )
            return total[:, :HALF]

        def subtract(engine, gap, value, carried):
            engine.tensor_tensor(out=gap, in0=value, in1=carried, op=ALU.subtract)

        def weigh(gap, tanh, difference):
            nc.vector.scalar_tensor_tensor(out=gap, in0=tanh, scalar=1.0, in1=difference, op0=ALU.add, op1=ALU.mult)

        def blend(carried, gap):
            nc.vector.scalar_tensor_tensor(out=carried, in0=gap, scalar=0.5, in1=carried, op0=ALU.mult, op1=ALU.add)

        def tanh_tile():
            return work.tile([P, 2 * CHUNK], F32, name="tanh")

        def gap_tile():
            return work.tile([P, 2 * CHUNK], F32, name="gap", bufs=2)

        tanh, gap = tanh_tile(), gap_tile()
        lower, upper = slice(0, HALF), slice(HALF, CHUNK)
        carried = stream[0][:, 0, :]
        round_x(0, nc.vector.tensor_copy)
        round_wg(0)
        quantize_x(0)
        value = value_branch(0, 0, HALF, 0)
        quantize_wg(0)
        spread_bias()
        gate_branch(0, 0, HALF, tanh[:, lower])
        round_x(1, nc.vector.tensor_copy)
        subtract(nc.vector, gap[:, lower], value[:, :HALF], carried[:, lower])
        quantize_x(1)
        round_wg(1)
        value = value_branch(0, HALF, HALF, 0)
        gate_branch(0, HALF, HALF, tanh[:, upper])
        weigh(gap[:, lower], tanh[:, lower], gap[:, lower])
        quantize_wg(1)
        blend(carried[:, lower], gap[:, lower])
        subtract(nc.vector, gap[:, upper], value[:, :HALF], carried[:, upper])
        last_carried, last_gap, last_tanh = carried[:, upper], gap[:, upper], tanh[:, upper]

        chunk1_start = len(FIRST_GROUPS) - 1
        chunk1_round = chunk1_start - 2
        chunk1_halves = (2, 3)
        chunk2_halves = (4, 5)
        summed_from = chunk1_start + len(chunk2_halves)
        minus_res = None
        last_terms = None

        for g, (c, b0, b1) in enumerate(groups):
            t0 = c * CHUNK
            blocks = range(b0, b1)
            upright_from = CHUNK - len(blocks) * CHUNK // 4
            turned = {b: upright_from if b == b0 else CHUNK for b in blocks}
            summed = g >= summed_from
            next_wg = b1 if c == 0 and b1 < BLOCKS else None

            values = {b: value_branch(b, t0, CHUNK, turned[b]) for b in blocks}
            if next_wg:
                round_wg(next_wg)
            if 0 <= g - chunk1_start < len(chunk2_halves):
                round_x(chunk2_halves[g - chunk1_start], nc.scalar.copy)
            tanh = tanh_tile()
            for b in blocks:
                gate_branch(b, t0, CHUNK, tanh[:, (b - b0) * CHUNK : (b - b0 + 1) * CHUNK])
            last_total = add_in_psum(*last_terms) if last_terms else None
            last_terms = (values[b0], minus_res) if summed else None
            if summed_from <= g + 1 < len(groups):
                minus_res = negate_res(*groups[g + 1][:2])
            on_vector = blocks[1:] if summed else blocks
            backs = {b: turn_back(values[b], turned[b]) for b in on_vector}

            if last_total is None:
                weigh(last_gap, last_tanh, last_gap)
            else:
                weigh(last_gap[:, HALF:], last_tanh[:, HALF:], last_gap[:, HALF:])
                weigh(last_gap[:, :HALF], last_tanh[:, :HALF], last_total)
            gap = gap_tile()
            carried = stream[c][:, b0:b1, :].rearrange("p b t -> p (b t)")
            upright = slice(upright_from, CHUNK)
            subtract(nc.gpsimd, gap[:, upright], values[b0][:, upright], carried[:, upright])
            for b in on_vector:
                cols = slice((b - b0) * CHUNK, (b - b0) * CHUNK + turned[b])
                subtract(nc.vector, gap[:, cols], backs[b][:, : turned[b]], carried[:, cols])
            if g == chunk1_round:
                for h in chunk1_halves:
                    round_x(h, nc.vector.tensor_copy)
                for h in chunk1_halves:
                    quantize_x(h)
            if 0 <= g - chunk1_start - 1 < len(chunk2_halves):
                quantize_x(chunk2_halves[g - chunk1_start - 1])
            if next_wg:
                quantize_wg(next_wg)
            blend(last_carried, last_gap)
            if g > 0:
                last_c, last_b0, last_b1 = groups[g - 1]
                store(last_c, last_b1 - 2, last_b1)
            width = len(blocks) * CHUNK
            last_carried, last_gap, last_tanh = carried, gap[:, :width], tanh[:, :width]

        weigh(last_gap[:, :HALF], last_tanh[:, :HALF], add_in_psum(*last_terms))
        weigh(last_gap[:, HALF:CHUNK], last_tanh[:, HALF:CHUNK], last_gap[:, HALF:CHUNK])
        pieces = ((0, 0, CHUNK), (1, 0, HALF), (1, HALF, HALF))
        spans = [slice(b * CHUNK + first, b * CHUNK + first + width) for b, first, width in pieces]
        for i, (b, first, width) in enumerate(pieces):
            if i + 1 < len(pieces):
                weigh(last_gap[:, spans[i + 1]], last_tanh[:, spans[i + 1]], last_gap[:, spans[i + 1]])
            blend(last_carried[:, spans[i]], last_gap[:, spans[i]])
            t0 = T - CHUNK + first
            nc.sync.dma_start(out=out_blocks[:, BLOCKS - 2 + b, t0 : t0 + width], in_=last_carried[:, spans[i]])
